import numpy as np
import ml_dtypes


def mxq(x, axis, fmt="e4m3"):
    dtype, down = {"e4m3": (ml_dtypes.float8_e4m3fn, 7), "e5m2": (ml_dtypes.float8_e5m2, 14)}[fmt]
    v = np.moveaxis(np.asarray(x, np.float32).astype(ml_dtypes.bfloat16).astype(np.float64), axis, -1)
    blocks = v.reshape(v.shape[:-1] + (-1, 32))
    amax = np.abs(blocks).max(-1, keepdims=True)
    byte = np.maximum(np.where(amax > 0, np.frexp(amax)[1] - 1 + 127, 0) - down, 1)
    scale = np.exp2(byte - 127.0)
    codes = (blocks / scale).astype(np.float32).astype(dtype).astype(np.float64)
    return np.moveaxis((codes * scale).reshape(v.shape), -1, axis)


WIDE = False


def mx_kscale(k):
    if not WIDE:
        return np.ones(k)
    levels = np.array([30, -30])
    if k % 512:
        return np.exp2(np.random.permutation(np.resize(levels, k // 32))).repeat(32)
    a = np.empty((k // 512, 16))
    for p in range(k // 512):
        a[p, :8] = np.random.permutation(np.resize(levels, 8))
        for g in range(8):
            far = levels[np.abs(levels - a[p, g]) >= 10]
            a[p, g + 8] = far[np.random.randint(len(far))]
    return np.exp2(a.ravel()).repeat(32)


def f64(x):
    return np.asarray(x).astype(np.float64)


def striped(idx):
    return np.tile(np.asarray(idx).reshape(-1, 16).T, (8, 1)).astype(np.uint16)


def unstriped(offs):
    return offs[:16].T.reshape(-1).astype(np.int64)


E2M1 = np.array([0.0, 0.5, 1.0, 1.5, 2.0, 3.0, 4.0, 6.0, -0.0, -0.5, -1.0, -1.5, -2.0, -3.0, -4.0, -6.0])


def pack_weight(w, fmt):
    k, n = w.shape
    w = f64(np.asarray(w, np.float32).astype(ml_dtypes.bfloat16)).reshape(k // 32, 32, n)
    amax = np.abs(w).max(1)
    if fmt == "e4m3":
        byte = np.frexp(amax)[1] - 1 + 127 - 7
    else:
        mant, ex = np.frexp(amax / 6.0)
        byte = np.where(mant > 0.5, ex, ex - 1) + 127
    byte = np.clip(np.where(amax > 0, byte, 1), 1, 254)
    scaled = (w * np.exp2(127.0 - byte)[:, None, :]).reshape(k, n).astype(np.float32)
    by_word = np.ascontiguousarray(scaled.reshape(k // 512, 128, 4, n).transpose(0, 1, 3, 2))
    if fmt == "e4m3":
        words = by_word.astype(ml_dtypes.float8_e4m3fn).view(np.uint8)
    else:
        c = by_word.astype(ml_dtypes.float4_e2m1fn).view(np.uint8) & 0xF
        words = (c[..., 0::2] | (c[..., 1::2] << 4)).reshape(k // 512, 128, 2 * n)
    return np.ascontiguousarray(words), np.ascontiguousarray(byte.astype(np.uint8).reshape(k // 512, 16, n))


def unpack_weight(words, scales, fmt):
    g, _, n = scales.shape
    words = np.ascontiguousarray(words).reshape(g, 128, n, -1)
    if fmt == "e4m3":
        vals = words.view(ml_dtypes.float8_e4m3fn).astype(np.float64)
    else:
        nib = np.empty((g, 128, n, 4), np.uint8)
        nib[..., 0::2] = words & 0xF
        nib[..., 1::2] = words >> 4
        vals = E2M1[nib]
    vals = vals * np.repeat(np.exp2(scales.astype(np.float64) - 127.0), 8, axis=1)[..., None]
    return vals.transpose(0, 1, 3, 2).reshape(g * 512, n)


T, K, V, N, J = 1024, 512, 1024, 512, 128


def setup_inputs():
    n = np.random.standard_normal
    idx = np.random.permutation(V)[:J]
    ft = mx_kscale(T)
    fn = mx_kscale(N)
    gp = pack_weight(n((N, J)) / fn[:, None], "e4m3")
    wp = pack_weight(n((N, K)) * 1 / np.sqrt(N) * fn[:, None], "e2m1")
    return {
        "h2": (n((T, K)) * ft[:, None]).astype(np.float32),
        "e": (n((T, V)) / ft[:, None]).astype(np.float32),
        "g_words": gp[0],
        "g_scales": gp[1],
        "w_words": wp[0],
        "w_scales": wp[1],
        "offs": striped(idx),
    }


def reference(h2, e, g_words, g_scales, w_words, w_scales, offs):
    idx = unstriped(offs)
    gu = unpack_weight(g_words, g_scales, "e4m3")
    wu = unpack_weight(w_words, w_scales, "e2m1")
    h2q = mxq(f64(h2), 0, "e4m3")
    eq = mxq(f64(e), 0, "e5m2")
    o = h2q.T @ eq
    dx = wu.T @ gu
    p = np.zeros((K, V))
    p[:, idx] = dx
    y = 0.03 * o + p
    return y

@@ -1,0 +1,192 @@
+from contextlib import ExitStack
+
+import concourse.mybir as mybir
+
+T, K, V, N, J = 1024, 512, 1024, 512, 128
+FLOPS = 2 * T * K * V + 2 * N * K * J
+
+F32 = mybir.dt.float32
+BF16 = mybir.dt.bfloat16
+I32 = mybir.dt.int32
+U32 = mybir.dt.uint32
+U16 = mybir.dt.uint16
+U8 = mybir.dt.uint8
+E4M3 = mybir.dt.float8_e4m3fn_x4
+E5M2 = mybir.dt.float8_e5m2_x4
+E2M1 = mybir.dt.float4_e2m1fn_x4
+MULT = mybir.AluOpType.mult
+ADD = mybir.AluOpType.add
+
+P = 128
+PACK = 4
+PASS = P * PACK
+BANK = 512
+ALPHA = 0.03
+
+
+def tile_list_tied_table_grad_kernel(tc, h2, e, g_words, g_scales, w_words, w_scales, offs, out):
+    nc = tc.nc
+    with ExitStack() as ctx:
+        keep = ctx.enter_context(tc.tile_pool(name="keep", bufs=1))
+        psum = ctx.enter_context(tc.psum_pool(name="psum", bufs=1))
+
+        pieces = [
+            ("h", 0, 0, 256, 0),
+            ("e", 0, 0, 512, 192),
+            ("h", 1, 0, 256, 256),
+            ("e", 1, 0, 512, 384),
+            ("e", 0, 512, 512, 384),
+            ("e", 1, 512, 256, 192),
+            ("e", 1, 768, 256, 192),
+            ("h", 0, 256, 256, 256),
+            ("h", 1, 256, 128, 128),
+            ("h", 1, 384, 128, 128),
+        ]
+        source = {"h": h2, "e": e}
+        fmt = {"h": E4M3, "e": E5M2}
+
+        g_plane = keep.tile([P, J], U8, name="g_plane", align_bytes=64)
+        w_plane = keep.tile([P, K], U8, name="w_plane", align_bytes=64)
+        nc.vector.memset(g_plane[:].bitcast(I32), 0)
+        nc.vector.memset(w_plane[:].bitcast(I32), 0)
+
+        warm = keep.tile([P, 16], F32, name="warm")
+        nc.vector.memset(warm[:, 0:8], 0.0)
+
+        def raw_tag(n):
+            if n < 2:
+                return "raw%d" % n
+            m = (n - 2) // 2
+            return raw_tag(m) if n % 2 == 0 else "woven%d" % m
+
+        raw = []
+        g_codes = keep.tile([P, 4 * J], U8, name="g_codes", align_bytes=64)
+        w_codes = keep.tile([P, 2 * K], U8, name="w_codes", align_bytes=64)
+        offsets = keep.tile([P, J // 16], U16, name="offsets")
+        def load(n):
+            who, a, c0, width, share = pieces[n]
+            tile = keep.tile([P, PACK, width], F32, name="raw%d" % n, tag=raw_tag(n), align_bytes=64)
+            rows = source[who][a * PASS : (a + 1) * PASS, c0 : c0 + width]
+            nc.sync.dma_start(out=tile[:], in_=rows.rearrange("(p j) w -> p j w", j=PACK))
+            raw.append(tile)
+            if n == 0:
+                nc.sync.dma_start(offsets[:], offs)
+                nc.sync.dma_start(out=g_codes[:].bitcast(I32), in_=g_words[0].rearrange("p c r -> p (c r)").bitcast(I32))
+                nc.sync.dma_start(out=w_codes[:].bitcast(I32), in_=w_words[0].bitcast(I32))
+                for q in range(4):
+                    if q == 2:
+                        nc.scalar.copy(out=warm[:, 8:16], in_=warm[:, 0:8])
+                    nc.scalar.dma_start(
+                        out=w_plane[32 * q : 32 * q + 4, :].bitcast(I32), in_=w_scales[0, 4 * q : 4 * q + 4, :].bitcast(I32)
+                    )
+                    nc.scalar.dma_start(
+                        out=g_plane[32 * q : 32 * q + 4, :].bitcast(I32), in_=g_scales[0, 4 * q : 4 * q + 4, :].bitcast(I32)
+                    )
+
+        load(0)
+        load(1)
+        placed = [keep.tile([P, V], F32, name="placed%d" % b) for b in range(K // P)]
+
+        codes = {}
+        planes = {}
+        for a in range(T // PASS):
+            for half in range(V // BANK):
+                codes["e", a, half] = keep.tile([P, BANK], U32, name="ec%d%d" % (a, half), align_bytes=64)
+                planes["e", a, half] = keep.tile([P, BANK], U8, name="ep%d%d" % (a, half), align_bytes=64)
+            for half in range(2):
+                codes["h", a, half] = keep.tile([P, 256], U32, name="hc%d%d" % (a, half), align_bytes=64)
+                planes["h", a, half] = keep.tile([P, 256], U8, name="hp%d%d" % (a, half), align_bytes=64)
+        span = {"h": 256, "e": BANK}
+
+        def prepare(n):
+            who, a, c0, width, share = pieces[n]
+            woven = keep.tile([P, width * PACK], BF16, name="woven%d" % n, tag="woven%d" % n, align_bytes=64)
+            for engine_copy, lo, hi in ((nc.scalar.copy, 0, share), (nc.vector.tensor_copy, share, width)):
+                if hi > lo:
+                    engine_copy(
+                        out=woven[:, lo * PACK : hi * PACK].rearrange("p (c i j) -> p c j i", i=4, j=PACK),
+                        in_=raw[n][:, :, lo:hi].rearrange("p j (c i) -> p c j i", i=4),
+                    )
+            key = (who, a, c0 // span[who])
+            cols = slice(c0 % span[who], c0 % span[who] + width)
+            nc.vector.quantize_mx(out=codes[key][:, cols].bitcast(fmt[who]), scales=planes[key][:, cols], in_=woven[:])
+            for later in (2 * n + 2, 2 * n + 3):
+                if later < len(pieces):
+                    load(later)
+
+        banks = {}
+
+        def multiply(b, half, a):
+            if a == 0:
+                tag = "bank%d" % ((2 * b + half + 1) % 8)
+                banks[b, half] = psum.tile([P, BANK], F32, name="o%d%d" % (b, half), tag=tag)
+            cols = slice((b % 2) * P, (b % 2 + 1) * P)
+            nc.tensor.matmul_mx(
+                out=banks[b, half][:],
+                lhsT=codes["h", a, b // 2][:, cols].bitcast(E4M3),
+                lhsT_scale=planes["h", a, b // 2][:, cols],
+                rhs=codes["e", a, half][:].bitcast(E5M2),
+                rhs_scale=planes["e", a, half][:],
+                start=(a == 0),
+                stop=(a == 1),
+            )
+
+        def finish(b, half):
+            cols = slice(half * BANK, (half + 1) * BANK)
+            result = keep.tile([P, BANK], F32, name="y%d%d" % (b, half))
+            nc.vector.scalar_tensor_tensor(
+                out=result[:], in0=banks[b, half][:], scalar=ALPHA, in1=placed[b][:, cols], op0=MULT, op1=ADD
+            )
+            nc.sync.dma_start(out=out[b * P : (b + 1) * P, cols], in_=result[:])
+
+        prepare(0)
+        for b in range(K // P):
+            nc.vector.memset(placed[b][:], 0.0)
+        dx_bank = psum.tile([P, K // P, J], F32, name="dx_bank", tag="bank0")
+        for b in range(K // P):
+            nc.tensor.matmul_mx(
+                out=dx_bank[:, b, :],
+                lhsT=w_codes[:, 2 * b * P : 2 * (b + 1) * P].bitcast(E2M1),
+                lhsT_scale=w_plane[:, b * P : (b + 1) * P],
+                rhs=g_codes[:].bitcast(E4M3),
+                rhs_scale=g_plane[:],
+                start=True,
+                stop=True,
+            )
+        dx = keep.tile([P, K // P, J], F32, name="dx")
+        nc.scalar.copy(out=dx[:], in_=dx_bank[:])
+        prepare(1)
+        multiply(0, 0, 0)
+        multiply(1, 0, 0)
+        for b in range(2):
+            nc.vector.tensor_copy(placed[b][:].indirect(offsets[:]), dx[:, b, :])
+        prepare(2)
+        prepare(3)
+        multiply(0, 0, 1)
+        multiply(1, 0, 1)
+        for b in range(2, 4):
+            nc.vector.tensor_copy(placed[b][:].indirect(offsets[:]), dx[:, b, :])
+        prepare(4)
+        multiply(0, 1, 0)
+        multiply(1, 1, 0)
+        finish(0, 0)
+        prepare(5)
+        finish(1, 0)
+        prepare(6)
+        multiply(0, 1, 1)
+        multiply(1, 1, 1)
+        prepare(7)
+        for b in (2, 3):
+            for half in range(2):
+                multiply(b, half, 0)
+        finish(0, 1)
+        prepare(8)
+        multiply(2, 0, 1)
+        multiply(2, 1, 1)
+        finish(1, 1)
+        prepare(9)
+        multiply(3, 0, 1)
+        multiply(3, 1, 1)
+        for b in (2, 3):
+            for half in range(2):
+                finish(b, half)

@@ -32,11 +32,13 @@ def tile_list_tied_table_grad_kernel(tc, h2, e, g_words, g_scales, w_words, w_sc
 
         pieces = [
             ("h", 0, 0, 256, 0),
-            ("e", 0, 0, 512, 192),
+            ("e", 0, 0, 512, 128),
             ("h", 1, 0, 256, 256),
-            ("e", 1, 0, 512, 384),
-            ("e", 0, 512, 512, 384),
-            ("e", 1, 512, 256, 192),
+            ("e", 1, 0, 256, 256),
+            ("e", 1, 256, 256, 256),
+            ("e", 0, 512, 256, 256),
+            ("e", 0, 768, 256, 256),
+            ("e", 1, 512, 256, 256),
             ("e", 1, 768, 256, 192),
             ("h", 0, 256, 256, 256),
             ("h", 1, 256, 128, 128),
@@ -49,42 +51,57 @@ def tile_list_tied_table_grad_kernel(tc, h2, e, g_words, g_scales, w_words, w_sc
         w_plane = keep.tile([P, K], U8, name="w_plane", align_bytes=64)
         nc.vector.memset(g_plane[:].bitcast(I32), 0)
         nc.vector.memset(w_plane[:].bitcast(I32), 0)
-
         warm = keep.tile([P, 16], F32, name="warm")
         nc.vector.memset(warm[:, 0:8], 0.0)
 
-        def raw_tag(n):
-            if n < 2:
-                return "raw%d" % n
-            m = (n - 2) // 2
-            return raw_tag(m) if n % 2 == 0 else "woven%d" % m
-
         raw = []
+        later = []
         g_codes = keep.tile([P, 4 * J], U8, name="g_codes", align_bytes=64)
         w_codes = keep.tile([P, 2 * K], U8, name="w_codes", align_bytes=64)
         offsets = keep.tile([P, J // 16], U16, name="offsets")
+
         def load(n):
             who, a, c0, width, share = pieces[n]
-            tile = keep.tile([P, PACK, width], F32, name="raw%d" % n, tag=raw_tag(n), align_bytes=64)
+            if n < 2:
+                tile = keep.tile([P, PACK * width], F32, name="raw%d" % n, tag="raw%d" % n)[:]
+            else:
+                first = PACK * sum(piece[3] for piece in pieces[2:n])
+                tile = later[0][:, first : first + PACK * width]
+            tile = tile.rearrange("p (j w) -> p j w", j=PACK)
             rows = source[who][a * PASS : (a + 1) * PASS, c0 : c0 + width]
-            nc.sync.dma_start(out=tile[:], in_=rows.rearrange("(p j) w -> p j w", j=PACK))
+            nc.sync.dma_start(out=tile, in_=rows.rearrange("(p j) w -> p j w", j=PACK))
             raw.append(tile)
-            if n == 0:
-                nc.sync.dma_start(offsets[:], offs)
-                nc.sync.dma_start(out=g_codes[:].bitcast(I32), in_=g_words[0].rearrange("p c r -> p (c r)").bitcast(I32))
-                nc.sync.dma_start(out=w_codes[:].bitcast(I32), in_=w_words[0].bitcast(I32))
-                for q in range(4):
-                    if q == 2:
-                        nc.scalar.copy(out=warm[:, 8:16], in_=warm[:, 0:8])
-                    nc.scalar.dma_start(
-                        out=w_plane[32 * q : 32 * q + 4, :].bitcast(I32), in_=w_scales[0, 4 * q : 4 * q + 4, :].bitcast(I32)
-                    )
-                    nc.scalar.dma_start(
-                        out=g_plane[32 * q : 32 * q + 4, :].bitcast(I32), in_=g_scales[0, 4 * q : 4 * q + 4, :].bitcast(I32)
-                    )
 
+        def scale_rows(queue, plane, scales, q):
+            queue.dma_start(out=plane[32 * q : 32 * q + 4, :].bitcast(I32), in_=scales[0, 4 * q : 4 * q + 4, :].bitcast(I32))
+
+        def offs_load():
+            nc.sync.dma_start(offsets[:], offs)
+
+        def g_load(queue):
+            queue.dma_start(out=g_codes[:].bitcast(I32), in_=g_words[0].rearrange("p c r -> p (c r)").bitcast(I32))
+
+        def w_load(queue):
+            queue.dma_start(out=w_codes[:].bitcast(I32), in_=w_words[0].bitcast(I32))
+
+        def warm_up():
+            nc.scalar.copy(out=warm[:, 8:16], in_=warm[:, 0:8])
+
+        offs_load()
+        g_load(nc.sync)
+        w_load(nc.sync)
         load(0)
         load(1)
+        scale_rows(nc.scalar, g_plane, g_scales, 0)
+        scale_rows(nc.scalar, g_plane, g_scales, 1)
+        scale_rows(nc.scalar, g_plane, g_scales, 2)
+        scale_rows(nc.scalar, g_plane, g_scales, 3)
+        scale_rows(nc.scalar, w_plane, w_scales, 0)
+        scale_rows(nc.scalar, w_plane, w_scales, 1)
+        scale_rows(nc.scalar, w_plane, w_scales, 2)
+        scale_rows(nc.scalar, w_plane, w_scales, 3)
+        warm_up()
+
         placed = [keep.tile([P, V], F32, name="placed%d" % b) for b in range(K // P)]
 
         codes = {}
@@ -93,98 +110,124 @@ def tile_list_tied_table_grad_kernel(tc, h2, e, g_words, g_scales, w_words, w_sc
             for half in range(V // BANK):
                 codes["e", a, half] = keep.tile([P, BANK], U32, name="ec%d%d" % (a, half), align_bytes=64)
                 planes["e", a, half] = keep.tile([P, BANK], U8, name="ep%d%d" % (a, half), align_bytes=64)
-            for half in range(2):
+            for half in range(K // 256):
                 codes["h", a, half] = keep.tile([P, 256], U32, name="hc%d%d" % (a, half), align_bytes=64)
                 planes["h", a, half] = keep.tile([P, 256], U8, name="hp%d%d" % (a, half), align_bytes=64)
         span = {"h": 256, "e": BANK}
+        woven = {}
 
-        def prepare(n):
+        def cast(n):
             who, a, c0, width, share = pieces[n]
-            woven = keep.tile([P, width * PACK], BF16, name="woven%d" % n, tag="woven%d" % n, align_bytes=64)
+            woven[n] = keep.tile([P, width * PACK], BF16, name="woven%d" % n, align_bytes=64)
             for engine_copy, lo, hi in ((nc.scalar.copy, 0, share), (nc.vector.tensor_copy, share, width)):
                 if hi > lo:
                     engine_copy(
-                        out=woven[:, lo * PACK : hi * PACK].rearrange("p (c i j) -> p c j i", i=4, j=PACK),
+                        out=woven[n][:, lo * PACK : hi * PACK].rearrange("p (c i j) -> p c j i", i=4, j=PACK),
                         in_=raw[n][:, :, lo:hi].rearrange("p j (c i) -> p c j i", i=4),
                     )
+
+        def quantize(n):
+            who, a, c0, width, share = pieces[n]
             key = (who, a, c0 // span[who])
             cols = slice(c0 % span[who], c0 % span[who] + width)
-            nc.vector.quantize_mx(out=codes[key][:, cols].bitcast(fmt[who]), scales=planes[key][:, cols], in_=woven[:])
-            for later in (2 * n + 2, 2 * n + 3):
-                if later < len(pieces):
-                    load(later)
+            nc.vector.quantize_mx(out=codes[key][:, cols].bitcast(fmt[who]), scales=planes[key][:, cols], in_=woven[n][:])
+
+        def prepare(n):
+            cast(n)
+            quantize(n)
 
         banks = {}
 
         def multiply(b, half, a):
-            if a == 0:
-                tag = "bank%d" % ((2 * b + half + 1) % 8)
+            if (b, half) not in banks:
+                tag = "bank%d" % ((len(banks) + 1) % 8)
                 banks[b, half] = psum.tile([P, BANK], F32, name="o%d%d" % (b, half), tag=tag)
-            cols = slice((b % 2) * P, (b % 2 + 1) * P)
+            per = span["h"] // P
+            cols = slice((b % per) * P, (b % per + 1) * P)
             nc.tensor.matmul_mx(
                 out=banks[b, half][:],
-                lhsT=codes["h", a, b // 2][:, cols].bitcast(E4M3),
-                lhsT_scale=planes["h", a, b // 2][:, cols],
+                lhsT=codes["h", a, b // per][:, cols].bitcast(E4M3),
+                lhsT_scale=planes["h", a, b // per][:, cols],
                 rhs=codes["e", a, half][:].bitcast(E5M2),
                 rhs_scale=planes["e", a, half][:],
                 start=(a == 0),
                 stop=(a == 1),
             )
 
-        def finish(b, half):
-            cols = slice(half * BANK, (half + 1) * BANK)
-            result = keep.tile([P, BANK], F32, name="y%d%d" % (b, half))
-            nc.vector.scalar_tensor_tensor(
-                out=result[:], in0=banks[b, half][:], scalar=ALPHA, in1=placed[b][:, cols], op0=MULT, op1=ADD
-            )
-            nc.sync.dma_start(out=out[b * P : (b + 1) * P, cols], in_=result[:])
+        def finish(b, half, queue=nc.sync, parts=1):
+            width = BANK // parts
+            for part in range(parts):
+                inner = slice(part * width, (part + 1) * width)
+                cols = slice(half * BANK + part * width, half * BANK + (part + 1) * width)
+                result = keep.tile([P, width], F32, name="y%d%d%d" % (b, half, part))
+                nc.vector.scalar_tensor_tensor(
+                    out=result[:], in0=banks[b, half][:, inner], scalar=ALPHA, in1=placed[b][:, cols], op0=MULT, op1=ADD
+                )
+                queue.dma_start(out=out[b * P : (b + 1) * P, cols], in_=result[:])
+
+        dx = keep.tile([P, K // P, J], F32, name="dx")
+
+        def backward():
+            dx_bank = psum.tile([P, K // P, J], F32, name="dx_bank", tag="bank0")
+            for b in range(K // P):
+                nc.tensor.matmul_mx(
+                    out=dx_bank[:, b, :],
+                    lhsT=w_codes[:, 2 * b * P : 2 * (b + 1) * P].bitcast(E2M1),
+                    lhsT_scale=w_plane[:, b * P : (b + 1) * P],
+                    rhs=g_codes[:].bitcast(E4M3),
+                    rhs_scale=g_plane[:],
+                    start=True,
+                    stop=True,
+                )
+            nc.scalar.copy(out=dx[:], in_=dx_bank[:])
+
+        def clear(b, engine):
+            engine.memset(placed[b][:], 0.0)
+
+        def scatter(b):
+            nc.vector.tensor_copy(placed[b][:].indirect(offsets[:]), dx[:, b, :])
 
         prepare(0)
-        for b in range(K // P):
-            nc.vector.memset(placed[b][:], 0.0)
-        dx_bank = psum.tile([P, K // P, J], F32, name="dx_bank", tag="bank0")
-        for b in range(K // P):
-            nc.tensor.matmul_mx(
-                out=dx_bank[:, b, :],
-                lhsT=w_codes[:, 2 * b * P : 2 * (b + 1) * P].bitcast(E2M1),
-                lhsT_scale=w_plane[:, b * P : (b + 1) * P],
-                rhs=g_codes[:].bitcast(E4M3),
-                rhs_scale=g_plane[:],
-                start=True,
-                stop=True,
-            )
-        dx = keep.tile([P, K // P, J], F32, name="dx")
-        nc.scalar.copy(out=dx[:], in_=dx_bank[:])
+        later.append(keep.tile([P, PACK * sum(piece[3] for piece in pieces[2:])], F32, name="later", tag="raw0"))
+        for n in range(2, len(pieces)):
+            load(n)
+        clear(0, nc.vector)
+        clear(1, nc.vector)
+        clear(2, nc.gpsimd)
+        clear(3, nc.gpsimd)
         prepare(1)
+        backward()
         multiply(0, 0, 0)
         multiply(1, 0, 0)
-        for b in range(2):
-            nc.vector.tensor_copy(placed[b][:].indirect(offsets[:]), dx[:, b, :])
         prepare(2)
+        scatter(0)
         prepare(3)
+        scatter(1)
+        prepare(4)
         multiply(0, 0, 1)
         multiply(1, 0, 1)
-        for b in range(2, 4):
-            nc.vector.tensor_copy(placed[b][:].indirect(offsets[:]), dx[:, b, :])
-        prepare(4)
+        scatter(2)
+        prepare(5)
+        scatter(3)
+        prepare(6)
         multiply(0, 1, 0)
         multiply(1, 1, 0)
         finish(0, 0)
-        prepare(5)
+        prepare(7)
         finish(1, 0)
-        prepare(6)
+        prepare(8)
         multiply(0, 1, 1)
         multiply(1, 1, 1)
-        prepare(7)
+        prepare(9)
         for b in (2, 3):
             for half in range(2):
                 multiply(b, half, 0)
         finish(0, 1)
-        prepare(8)
+        prepare(10)
         multiply(2, 0, 1)
         multiply(2, 1, 1)
         finish(1, 1)
-        prepare(9)
+        prepare(11)
         multiply(3, 0, 1)
         multiply(3, 1, 1)
         for b in (2, 3):

@@ -34,12 +34,10 @@ def tile_list_tied_table_grad_kernel(tc, h2, e, g_words, g_scales, w_words, w_sc
             ("h", 0, 0, 256, 0),
             ("e", 0, 0, 512, 128),
             ("h", 1, 0, 256, 256),
-            ("e", 1, 0, 256, 256),
-            ("e", 1, 256, 256, 256),
-            ("e", 0, 512, 256, 256),
-            ("e", 0, 768, 256, 256),
+            ("e", 1, 0, 512, 384),
+            ("e", 0, 512, 512, 384),
             ("e", 1, 512, 256, 256),
-            ("e", 1, 768, 256, 192),
+            ("e", 1, 768, 256, 128),
             ("h", 0, 256, 256, 256),
             ("h", 1, 256, 128, 128),
             ("h", 1, 384, 128, 128),
@@ -122,8 +120,8 @@ def tile_list_tied_table_grad_kernel(tc, h2, e, g_words, g_scales, w_words, w_sc
             for engine_copy, lo, hi in ((nc.scalar.copy, 0, share), (nc.vector.tensor_copy, share, width)):
                 if hi > lo:
                     engine_copy(
-                        out=woven[n][:, lo * PACK : hi * PACK].rearrange("p (c i j) -> p c j i", i=4, j=PACK),
-                        in_=raw[n][:, :, lo:hi].rearrange("p j (c i) -> p c j i", i=4),
+                        out=woven[n][:, lo * PACK : hi * PACK].rearrange("p (c j) -> p c j", j=PACK),
+                        in_=raw[n][:, :, lo:hi].rearrange("p j c -> p c j"),
                     )
 
         def quantize(n):
@@ -195,41 +193,38 @@ def tile_list_tied_table_grad_kernel(tc, h2, e, g_words, g_scales, w_words, w_sc
         clear(1, nc.vector)
         clear(2, nc.gpsimd)
         clear(3, nc.gpsimd)
-        prepare(1)
         backward()
+        prepare(1)
         multiply(0, 0, 0)
         multiply(1, 0, 0)
         prepare(2)
-        scatter(0)
         prepare(3)
-        scatter(1)
-        prepare(4)
         multiply(0, 0, 1)
         multiply(1, 0, 1)
+        scatter(0)
+        scatter(1)
         scatter(2)
-        prepare(5)
         scatter(3)
-        prepare(6)
+        prepare(4)
         multiply(0, 1, 0)
         multiply(1, 1, 0)
-        finish(0, 0)
-        prepare(7)
-        finish(1, 0)
-        prepare(8)
+        prepare(5)
+        prepare(6)
         multiply(0, 1, 1)
         multiply(1, 1, 1)
-        prepare(9)
+        prepare(7)
         for b in (2, 3):
             for half in range(2):
                 multiply(b, half, 0)
-        finish(0, 1)
-        prepare(10)
+        prepare(8)
         multiply(2, 0, 1)
         multiply(2, 1, 1)
-        finish(1, 1)
-        prepare(11)
+        prepare(9)
         multiply(3, 0, 1)
         multiply(3, 1, 1)
+        for half in range(2):
+            for b in (0, 1):
+                finish(b, half)
         for b in (2, 3):
             for half in range(2):
                 finish(b, half)

@@ -4,6 +4,7 @@ import concourse.mybir as mybir
 
 T, K, V, N, J = 1024, 512, 1024, 512, 128
 FLOPS = 2 * T * K * V + 2 * N * K * J
+ALPHA = 0.03
 
 F32 = mybir.dt.float32
 BF16 = mybir.dt.bfloat16
@@ -20,211 +21,163 @@ ADD = mybir.AluOpType.add
 P = 128
 PACK = 4
 PASS = P * PACK
+PASSES = T // PASS
 BANK = 512
-ALPHA = 0.03
+BANKS = 8
+ROW_BLOCKS = K // P
+QUADRANTS = 4
+H_SPAN = 2 * P
+RUN = 4
+
+PIECES = [
+    ("h", 0, 0, 256, 0),
+    ("e", 0, 0, 512, 128),
+    ("h", 1, 0, 256, 256),
+    ("e", 1, 0, 512, 512),
+    ("h", 0, 256, 256, 256),
+    ("h", 1, 256, 256, 256),
+    ("e", 0, 512, 512, 512),
+    ("e", 1, 512, 256, 256),
+    ("e", 1, 768, 256, 128),
+]
+FIRST_LOADS = 2
 
 
 def tile_list_tied_table_grad_kernel(tc, h2, e, g_words, g_scales, w_words, w_scales, offs, out):
     nc = tc.nc
+    source = {"h": h2, "e": e}
+    mx_format = {"h": E4M3, "e": E5M2}
+    span = {"h": H_SPAN, "e": BANK}
+
     with ExitStack() as ctx:
         keep = ctx.enter_context(tc.tile_pool(name="keep", bufs=1))
         psum = ctx.enter_context(tc.psum_pool(name="psum", bufs=1))
-
-        pieces = [
-            ("h", 0, 0, 256, 0),
-            ("e", 0, 0, 512, 128),
-            ("h", 1, 0, 256, 256),
-            ("e", 1, 0, 512, 384),
-            ("e", 0, 512, 512, 384),
-            ("e", 1, 512, 256, 256),
-            ("e", 1, 768, 256, 128),
-            ("h", 0, 256, 256, 256),
-            ("h", 1, 256, 128, 128),
-            ("h", 1, 384, 128, 128),
-        ]
-        source = {"h": h2, "e": e}
-        fmt = {"h": E4M3, "e": E5M2}
 
         g_plane = keep.tile([P, J], U8, name="g_plane", align_bytes=64)
         w_plane = keep.tile([P, K], U8, name="w_plane", align_bytes=64)
         nc.vector.memset(g_plane[:].bitcast(I32), 0)
         nc.vector.memset(w_plane[:].bitcast(I32), 0)
-        warm = keep.tile([P, 16], F32, name="warm")
-        nc.vector.memset(warm[:, 0:8], 0.0)
 
-        raw = []
-        later = []
         g_codes = keep.tile([P, 4 * J], U8, name="g_codes", align_bytes=64)
         w_codes = keep.tile([P, 2 * K], U8, name="w_codes", align_bytes=64)
         offsets = keep.tile([P, J // 16], U16, name="offsets")
 
-        def load(n):
-            who, a, c0, width, share = pieces[n]
-            if n < 2:
-                tile = keep.tile([P, PACK * width], F32, name="raw%d" % n, tag="raw%d" % n)[:]
-            else:
-                first = PACK * sum(piece[3] for piece in pieces[2:n])
-                tile = later[0][:, first : first + PACK * width]
-            tile = tile.rearrange("p (j w) -> p j w", j=PACK)
-            rows = source[who][a * PASS : (a + 1) * PASS, c0 : c0 + width]
-            nc.sync.dma_start(out=tile, in_=rows.rearrange("(p j) w -> p j w", j=PACK))
-            raw.append(tile)
+        raw = []
 
-        def scale_rows(queue, plane, scales, q):
-            queue.dma_start(out=plane[32 * q : 32 * q + 4, :].bitcast(I32), in_=scales[0, 4 * q : 4 * q + 4, :].bitcast(I32))
+        def load(n, staging):
+            operand, a, first, width, scalar_columns = PIECES[n]
+            rows = source[operand][a * PASS : (a + 1) * PASS, first : first + width]
+            raw.append(staging.rearrange("p (i c) -> p i c", i=PACK))
+            nc.sync.dma_start(out=raw[n], in_=rows.rearrange("(p i) c -> p i c", i=PACK))
 
-        def offs_load():
-            nc.sync.dma_start(offsets[:], offs)
+        nc.sync.dma_start(offsets[:], offs)
+        nc.sync.dma_start(out=g_codes[:].bitcast(I32), in_=g_words[0].rearrange("p c r -> p (c r)").bitcast(I32))
+        nc.sync.dma_start(out=w_codes[:].bitcast(I32), in_=w_words[0].bitcast(I32))
+        for n in range(FIRST_LOADS):
+            staging = keep.tile([P, PACK * PIECES[n][3]], F32, name="raw%d" % n, tag="raw%d" % n)
+            load(n, staging[:])
+        for plane, scales in ((g_plane, g_scales), (w_plane, w_scales)):
+            for q in range(QUADRANTS):
+                nc.scalar.dma_start(
+                    out=plane[32 * q : 32 * q + 4, :].bitcast(I32),
+                    in_=scales[0, 4 * q : 4 * q + 4, :].bitcast(I32),
+                )
 
-        def g_load(queue):
-            queue.dma_start(out=g_codes[:].bitcast(I32), in_=g_words[0].rearrange("p c r -> p (c r)").bitcast(I32))
-
-        def w_load(queue):
-            queue.dma_start(out=w_codes[:].bitcast(I32), in_=w_words[0].bitcast(I32))
-
-        def warm_up():
-            nc.scalar.copy(out=warm[:, 8:16], in_=warm[:, 0:8])
-
-        offs_load()
-        g_load(nc.sync)
-        w_load(nc.sync)
-        load(0)
-        load(1)
-        scale_rows(nc.scalar, g_plane, g_scales, 0)
-        scale_rows(nc.scalar, g_plane, g_scales, 1)
-        scale_rows(nc.scalar, g_plane, g_scales, 2)
-        scale_rows(nc.scalar, g_plane, g_scales, 3)
-        scale_rows(nc.scalar, w_plane, w_scales, 0)
-        scale_rows(nc.scalar, w_plane, w_scales, 1)
-        scale_rows(nc.scalar, w_plane, w_scales, 2)
-        scale_rows(nc.scalar, w_plane, w_scales, 3)
-        warm_up()
-
-        placed = [keep.tile([P, V], F32, name="placed%d" % b) for b in range(K // P)]
+        placed = [keep.tile([P, V], F32, name="placed%d" % b) for b in range(ROW_BLOCKS)]
 
         codes = {}
         planes = {}
-        for a in range(T // PASS):
+        for a in range(PASSES):
             for half in range(V // BANK):
                 codes["e", a, half] = keep.tile([P, BANK], U32, name="ec%d%d" % (a, half), align_bytes=64)
                 planes["e", a, half] = keep.tile([P, BANK], U8, name="ep%d%d" % (a, half), align_bytes=64)
-            for half in range(K // 256):
-                codes["h", a, half] = keep.tile([P, 256], U32, name="hc%d%d" % (a, half), align_bytes=64)
-                planes["h", a, half] = keep.tile([P, 256], U8, name="hp%d%d" % (a, half), align_bytes=64)
-        span = {"h": 256, "e": BANK}
-        woven = {}
-
-        def cast(n):
-            who, a, c0, width, share = pieces[n]
-            woven[n] = keep.tile([P, width * PACK], BF16, name="woven%d" % n, align_bytes=64)
-            for engine_copy, lo, hi in ((nc.scalar.copy, 0, share), (nc.vector.tensor_copy, share, width)):
-                if hi > lo:
-                    engine_copy(
-                        out=woven[n][:, lo * PACK : hi * PACK].rearrange("p (c j) -> p c j", j=PACK),
-                        in_=raw[n][:, :, lo:hi].rearrange("p j c -> p c j"),
-                    )
+            for pair in range(K // H_SPAN):
+                codes["h", a, pair] = keep.tile([P, H_SPAN], U32, name="hc%d%d" % (a, pair), align_bytes=64)
+                planes["h", a, pair] = keep.tile([P, H_SPAN], U8, name="hp%d%d" % (a, pair), align_bytes=64)
 
         def quantize(n):
-            who, a, c0, width, share = pieces[n]
-            key = (who, a, c0 // span[who])
-            cols = slice(c0 % span[who], c0 % span[who] + width)
-            nc.vector.quantize_mx(out=codes[key][:, cols].bitcast(fmt[who]), scales=planes[key][:, cols], in_=woven[n][:])
+            operand, a, first, width, scalar_columns = PIECES[n]
+            woven = keep.tile([P, width * PACK], BF16, name="woven%d" % n, align_bytes=64)
+            for copy, lo, hi in ((nc.scalar.copy, 0, scalar_columns), (nc.vector.tensor_copy, scalar_columns, width)):
+                if hi > lo:
+                    copy(
+                        out=woven[:, lo * PACK : hi * PACK].rearrange("p (c s i) -> p c i s", s=RUN, i=PACK),
+                        in_=raw[n][:, :, lo:hi].rearrange("p i (c s) -> p c i s", s=RUN),
+                    )
+            key = (operand, a, first // span[operand])
+            cols = slice(first % span[operand], first % span[operand] + width)
+            nc.vector.quantize_mx(
+                out=codes[key][:, cols].bitcast(mx_format[operand]), scales=planes[key][:, cols], in_=woven[:]
+            )
 
-        def prepare(n):
-            cast(n)
-            quantize(n)
-
-        banks = {}
+        sums = {}
 
         def multiply(b, half, a):
-            if (b, half) not in banks:
-                tag = "bank%d" % ((len(banks) + 1) % 8)
-                banks[b, half] = psum.tile([P, BANK], F32, name="o%d%d" % (b, half), tag=tag)
-            per = span["h"] // P
-            cols = slice((b % per) * P, (b % per + 1) * P)
+            if a == 0:
+                tag = "bank%d" % ((len(sums) + 1) % BANKS)
+                sums[b, half] = psum.tile([P, BANK], F32, name="o%d%d" % (b, half), tag=tag)
+            pair, member = divmod(b * P, H_SPAN)
+            cols = slice(member, member + P)
             nc.tensor.matmul_mx(
-                out=banks[b, half][:],
-                lhsT=codes["h", a, b // per][:, cols].bitcast(E4M3),
-                lhsT_scale=planes["h", a, b // per][:, cols],
+                out=sums[b, half][:],
+                lhsT=codes["h", a, pair][:, cols].bitcast(E4M3),
+                lhsT_scale=planes["h", a, pair][:, cols],
                 rhs=codes["e", a, half][:].bitcast(E5M2),
                 rhs_scale=planes["e", a, half][:],
                 start=(a == 0),
-                stop=(a == 1),
+                stop=(a == PASSES - 1),
             )
 
-        def finish(b, half, queue=nc.sync, parts=1):
-            width = BANK // parts
-            for part in range(parts):
-                inner = slice(part * width, (part + 1) * width)
-                cols = slice(half * BANK + part * width, half * BANK + (part + 1) * width)
-                result = keep.tile([P, width], F32, name="y%d%d%d" % (b, half, part))
-                nc.vector.scalar_tensor_tensor(
-                    out=result[:], in0=banks[b, half][:, inner], scalar=ALPHA, in1=placed[b][:, cols], op0=MULT, op1=ADD
-                )
-                queue.dma_start(out=out[b * P : (b + 1) * P, cols], in_=result[:])
+        dx = keep.tile([P, ROW_BLOCKS, J], F32, name="dx")
 
-        dx = keep.tile([P, K // P, J], F32, name="dx")
+        quantize(0)
 
-        def backward():
-            dx_bank = psum.tile([P, K // P, J], F32, name="dx_bank", tag="bank0")
-            for b in range(K // P):
-                nc.tensor.matmul_mx(
-                    out=dx_bank[:, b, :],
-                    lhsT=w_codes[:, 2 * b * P : 2 * (b + 1) * P].bitcast(E2M1),
-                    lhsT_scale=w_plane[:, b * P : (b + 1) * P],
-                    rhs=g_codes[:].bitcast(E4M3),
-                    rhs_scale=g_plane[:],
-                    start=True,
-                    stop=True,
-                )
-            nc.scalar.copy(out=dx[:], in_=dx_bank[:])
+        later = keep.tile([P, PACK * sum(piece[3] for piece in PIECES[FIRST_LOADS:])], F32, name="later", tag="raw0")
+        for n in range(FIRST_LOADS, len(PIECES)):
+            start = PACK * sum(piece[3] for piece in PIECES[FIRST_LOADS:n])
+            load(n, later[:, start : start + PACK * PIECES[n][3]])
 
-        def clear(b, engine):
-            engine.memset(placed[b][:], 0.0)
+        for b in range(ROW_BLOCKS):
+            nc.vector.memset(placed[b][:], 0.0)
 
-        def scatter(b):
+        dx_bank = psum.tile([P, ROW_BLOCKS, J], F32, name="dx_bank", tag="bank0")
+        for b in range(ROW_BLOCKS):
+            nc.tensor.matmul_mx(
+                out=dx_bank[:, b, :],
+                lhsT=w_codes[:, 2 * b * P : 2 * (b + 1) * P].bitcast(E2M1),
+                lhsT_scale=w_plane[:, b * P : (b + 1) * P],
+                rhs=g_codes[:].bitcast(E4M3),
+                rhs_scale=g_plane[:],
+                start=True,
+                stop=True,
+            )
+        nc.vector.tensor_copy(out=dx[:], in_=dx_bank[:])
+
+        columns_done = {("h", 0, 0): PIECES[0][3]}
+        multiplied = set()
+        for n in range(1, len(PIECES)):
+            quantize(n)
+            operand, a, first, width, scalar_columns = PIECES[n]
+            key = (operand, a, first // span[operand])
+            columns_done[key] = columns_done.get(key, 0) + width
+            for half in range(V // BANK):
+                for b in range(ROW_BLOCKS):
+                    ready = (
+                        columns_done.get(("h", a, b * P // H_SPAN), 0) == H_SPAN
+                        and columns_done.get(("e", a, half), 0) == BANK
+                    )
+                    if ready and (b, half, a) not in multiplied:
+                        multiplied.add((b, half, a))
+                        multiply(b, half, a)
+
+        for b in range(ROW_BLOCKS):
             nc.vector.tensor_copy(placed[b][:].indirect(offsets[:]), dx[:, b, :])
 
-        prepare(0)
-        later.append(keep.tile([P, PACK * sum(piece[3] for piece in pieces[2:])], F32, name="later", tag="raw0"))
-        for n in range(2, len(pieces)):
-            load(n)
-        clear(0, nc.vector)
-        clear(1, nc.vector)
-        clear(2, nc.gpsimd)
-        clear(3, nc.gpsimd)
-        backward()
-        prepare(1)
-        multiply(0, 0, 0)
-        multiply(1, 0, 0)
-        prepare(2)
-        prepare(3)
-        multiply(0, 0, 1)
-        multiply(1, 0, 1)
-        scatter(0)
-        scatter(1)
-        scatter(2)
-        scatter(3)
-        prepare(4)
-        multiply(0, 1, 0)
-        multiply(1, 1, 0)
-        prepare(5)
-        prepare(6)
-        multiply(0, 1, 1)
-        multiply(1, 1, 1)
-        prepare(7)
-        for b in (2, 3):
-            for half in range(2):
-                multiply(b, half, 0)
-        prepare(8)
-        multiply(2, 0, 1)
-        multiply(2, 1, 1)
-        prepare(9)
-        multiply(3, 0, 1)
-        multiply(3, 1, 1)
-        for half in range(2):
-            for b in (0, 1):
-                finish(b, half)
-        for b in (2, 3):
-            for half in range(2):
-                finish(b, half)
+        for half in range(V // BANK):
+            cols = slice(half * BANK, (half + 1) * BANK)
+            for b in range(ROW_BLOCKS):
+                result = keep.tile([P, BANK], F32, name="y%d%d" % (b, half))
+                nc.vector.scalar_tensor_tensor(
+                    out=result[:], in0=sums[b, half][:], scalar=ALPHA, in1=placed[b][:, cols], op0=MULT, op1=ADD
+                )
+                nc.sync.dma_start(out=out[b * P : (b + 1) * P, cols], in_=result[:])

from contextlib import ExitStack

import concourse.mybir as mybir

T, K, V, N, J = 1024, 512, 1024, 512, 128
FLOPS = 2 * T * K * V + 2 * N * K * J
ALPHA = 0.03

F32 = mybir.dt.float32
BF16 = mybir.dt.bfloat16
I32 = mybir.dt.int32
U32 = mybir.dt.uint32
U16 = mybir.dt.uint16
U8 = mybir.dt.uint8
E4M3 = mybir.dt.float8_e4m3fn_x4
E5M2 = mybir.dt.float8_e5m2_x4
E2M1 = mybir.dt.float4_e2m1fn_x4
MULT = mybir.AluOpType.mult
ADD = mybir.AluOpType.add

P = 128
PACK = 4
PASS = P * PACK
PASSES = T // PASS
BANK = 512
BANKS = 8
ROW_BLOCKS = K // P
QUADRANTS = 4
H_SPAN = 2 * P
RUN = 4

PIECES = [
    ("h", 0, 0, 256, 0),
    ("e", 0, 0, 512, 128),
    ("h", 1, 0, 256, 256),
    ("e", 1, 0, 512, 512),
    ("h", 0, 256, 256, 256),
    ("h", 1, 256, 256, 256),
    ("e", 0, 512, 512, 512),
    ("e", 1, 512, 256, 256),
    ("e", 1, 768, 256, 128),
]
FIRST_LOADS = 2


def tile_list_tied_table_grad_kernel(tc, h2, e, g_words, g_scales, w_words, w_scales, offs, out):
    nc = tc.nc
    source = {"h": h2, "e": e}
    mx_format = {"h": E4M3, "e": E5M2}
    span = {"h": H_SPAN, "e": BANK}

    with ExitStack() as ctx:
        keep = ctx.enter_context(tc.tile_pool(name="keep", bufs=1))
        psum = ctx.enter_context(tc.psum_pool(name="psum", bufs=1))

        g_plane = keep.tile([P, J], U8, name="g_plane", align_bytes=64)
        w_plane = keep.tile([P, K], U8, name="w_plane", align_bytes=64)
        nc.vector.memset(g_plane[:].bitcast(I32), 0)
        nc.vector.memset(w_plane[:].bitcast(I32), 0)

        g_codes = keep.tile([P, 4 * J], U8, name="g_codes", align_bytes=64)
        w_codes = keep.tile([P, 2 * K], U8, name="w_codes", align_bytes=64)
        offsets = keep.tile([P, J // 16], U16, name="offsets")

        raw = []

        def load(n, staging):
            operand, a, first, width, scalar_columns = PIECES[n]
            rows = source[operand][a * PASS : (a + 1) * PASS, first : first + width]
            raw.append(staging.rearrange("p (i c) -> p i c", i=PACK))
            nc.sync.dma_start(out=raw[n], in_=rows.rearrange("(p i) c -> p i c", i=PACK))

        nc.sync.dma_start(offsets[:], offs)
        nc.sync.dma_start(out=g_codes[:].bitcast(I32), in_=g_words[0].rearrange("p c r -> p (c r)").bitcast(I32))
        nc.sync.dma_start(out=w_codes[:].bitcast(I32), in_=w_words[0].bitcast(I32))
        for n in range(FIRST_LOADS):
            staging = keep.tile([P, PACK * PIECES[n][3]], F32, name="raw%d" % n, tag="raw%d" % n)
            load(n, staging[:])
        for plane, scales in ((g_plane, g_scales), (w_plane, w_scales)):
            for q in range(QUADRANTS):
                nc.scalar.dma_start(
                    out=plane[32 * q : 32 * q + 4, :].bitcast(I32),
                    in_=scales[0, 4 * q : 4 * q + 4, :].bitcast(I32),
                )

        placed = [keep.tile([P, V], F32, name="placed%d" % b) for b in range(ROW_BLOCKS)]

        codes = {}
        planes = {}
        for a in range(PASSES):
            for half in range(V // BANK):
                codes["e", a, half] = keep.tile([P, BANK], U32, name="ec%d%d" % (a, half), align_bytes=64)
                planes["e", a, half] = keep.tile([P, BANK], U8, name="ep%d%d" % (a, half), align_bytes=64)
            for pair in range(K // H_SPAN):
                codes["h", a, pair] = keep.tile([P, H_SPAN], U32, name="hc%d%d" % (a, pair), align_bytes=64)
                planes["h", a, pair] = keep.tile([P, H_SPAN], U8, name="hp%d%d" % (a, pair), align_bytes=64)

        def quantize(n):
            operand, a, first, width, scalar_columns = PIECES[n]
            woven = keep.tile([P, width * PACK], BF16, name="woven%d" % n, align_bytes=64)
            for copy, lo, hi in ((nc.scalar.copy, 0, scalar_columns), (nc.vector.tensor_copy, scalar_columns, width)):
                if hi > lo:
                    copy(
                        out=woven[:, lo * PACK : hi * PACK].rearrange("p (c s i) -> p c i s", s=RUN, i=PACK),
                        in_=raw[n][:, :, lo:hi].rearrange("p i (c s) -> p c i s", s=RUN),
                    )
            key = (operand, a, first // span[operand])
            cols = slice(first % span[operand], first % span[operand] + width)
            nc.vector.quantize_mx(
                out=codes[key][:, cols].bitcast(mx_format[operand]), scales=planes[key][:, cols], in_=woven[:]
            )

        sums = {}

        def multiply(b, half, a):
            if a == 0:
                tag = "bank%d" % ((len(sums) + 1) % BANKS)
                sums[b, half] = psum.tile([P, BANK], F32, name="o%d%d" % (b, half), tag=tag)
            pair, member = divmod(b * P, H_SPAN)
            cols = slice(member, member + P)
            nc.tensor.matmul_mx(
                out=sums[b, half][:],
                lhsT=codes["h", a, pair][:, cols].bitcast(E4M3),
                lhsT_scale=planes["h", a, pair][:, cols],
                rhs=codes["e", a, half][:].bitcast(E5M2),
                rhs_scale=planes["e", a, half][:],
                start=(a == 0),
                stop=(a == PASSES - 1),
            )

        dx = keep.tile([P, ROW_BLOCKS, J], F32, name="dx")

        quantize(0)

        later = keep.tile([P, PACK * sum(piece[3] for piece in PIECES[FIRST_LOADS:])], F32, name="later", tag="raw0")
        for n in range(FIRST_LOADS, len(PIECES)):
            start = PACK * sum(piece[3] for piece in PIECES[FIRST_LOADS:n])
            load(n, later[:, start : start + PACK * PIECES[n][3]])

        for b in range(ROW_BLOCKS):
            nc.vector.memset(placed[b][:], 0.0)

        dx_bank = psum.tile([P, ROW_BLOCKS, J], F32, name="dx_bank", tag="bank0")
        for b in range(ROW_BLOCKS):
            nc.tensor.matmul_mx(
                out=dx_bank[:, b, :],
                lhsT=w_codes[:, 2 * b * P : 2 * (b + 1) * P].bitcast(E2M1),
                lhsT_scale=w_plane[:, b * P : (b + 1) * P],
                rhs=g_codes[:].bitcast(E4M3),
                rhs_scale=g_plane[:],
                start=True,
                stop=True,
            )
        nc.vector.tensor_copy(out=dx[:], in_=dx_bank[:])

        columns_done = {("h", 0, 0): PIECES[0][3]}
        multiplied = set()
        for n in range(1, len(PIECES)):
            quantize(n)
            operand, a, first, width, scalar_columns = PIECES[n]
            key = (operand, a, first // span[operand])
            columns_done[key] = columns_done.get(key, 0) + width
            for half in range(V // BANK):
                for b in range(ROW_BLOCKS):
                    ready = (
                        columns_done.get(("h", a, b * P // H_SPAN), 0) == H_SPAN
                        and columns_done.get(("e", a, half), 0) == BANK
                    )
                    if ready and (b, half, a) not in multiplied:
                        multiplied.add((b, half, a))
                        multiply(b, half, a)

        for b in range(ROW_BLOCKS):
            nc.vector.tensor_copy(placed[b][:].indirect(offsets[:]), dx[:, b, :])

        for half in range(V // BANK):
            cols = slice(half * BANK, (half + 1) * BANK)
            for b in range(ROW_BLOCKS):
                result = keep.tile([P, BANK], F32, name="y%d%d" % (b, half))
                nc.vector.scalar_tensor_tensor(
                    out=result[:], in0=sums[b, half][:], scalar=ALPHA, in1=placed[b][:, cols], op0=MULT, op1=ADD
                )
                nc.sync.dma_start(out=out[b * P : (b + 1) * P, cols], in_=result[:])
